import numpy as np
import ml_dtypes


def mxq(x, axis, fmt="e4m3"):
    dtype, down = {"e4m3": (ml_dtypes.float8_e4m3fn, 7), "e5m2": (ml_dtypes.float8_e5m2, 14)}[fmt]
    v = np.moveaxis(np.asarray(x, np.float32).astype(ml_dtypes.bfloat16).astype(np.float64), axis, -1)
    blocks = v.reshape(v.shape[:-1] + (-1, 32))
    amax = np.abs(blocks).max(-1, keepdims=True)
    byte = np.maximum(np.where(amax > 0, np.frexp(amax)[1] - 1 + 127, 0) - down, 1)
    scale = np.exp2(byte - 127.0)
    codes = (blocks / scale).astype(np.float32).astype(dtype).astype(np.float64)
    return np.moveaxis((codes * scale).reshape(v.shape), -1, axis)


WIDE = False


def mx_kscale(k):
    if not WIDE:
        return np.ones(k)
    levels = np.array([10, -10, 5, -5, 0])
    if k % 512:
        return np.exp2(np.random.permutation(np.resize(levels, k // 32))).repeat(32)
    a = np.empty((k // 512, 16))
    for p in range(k // 512):
        a[p, :8] = np.random.permutation(np.resize(levels, 8))
        for g in range(8):
            far = levels[np.abs(levels - a[p, g]) >= 10]
            a[p, g + 8] = far[np.random.randint(len(far))]
    return np.exp2(a.ravel()).repeat(32)


def f64(x):
    return np.asarray(x).astype(np.float64)


def striped(idx):
    return np.tile(idx.reshape(-1, 16).T, (8, 1)).astype(np.uint16)


def unstriped(offs):
    return offs[:16].T.reshape(-1).astype(np.int64)


def pack_weight(w):
    k, n = w.shape
    w = f64(np.asarray(w, np.float32).astype(ml_dtypes.bfloat16)).reshape(k // 32, 32, n)
    amax = np.abs(w).max(1)
    byte = np.clip(np.where(amax > 0, np.frexp(amax)[1] - 1 + 127 - 7, 1), 1, 254)
    scaled = (w * np.exp2(127.0 - byte)[:, None, :]).reshape(k, n).astype(np.float32)
    words = np.ascontiguousarray(scaled.reshape(k // 512, 128, 4, n).transpose(0, 1, 3, 2)).astype(ml_dtypes.float8_e4m3fn).view(np.uint8)
    return words, np.ascontiguousarray(byte.astype(np.uint8).reshape(k // 512, 16, n))


def unpack_weight(words, scales):
    g, p, n, _ = words.shape
    vals = np.ascontiguousarray(words).view(ml_dtypes.float8_e4m3fn).astype(np.float64) * np.repeat(np.exp2(scales.astype(np.float64) - 127.0), 8, axis=1)[..., None]
    return vals.transpose(0, 1, 3, 2).reshape(g * 512, n)


K, T, N = 512, 1024, 128
P = 2 ** 7


def setup_inputs():
    n = np.random.standard_normal
    s = mx_kscale(K)[:, None]
    packed_xT = pack_weight(n((K, T)) * s)
    return {
        "x_words": packed_xT[0],
        "x_scales": packed_xT[1],
        "w1": (n((K, N)) / np.sqrt(K) / s).astype(np.float32),
        "fx": np.tile(np.random.uniform(0.05, 0.95, T), (P, 1)).astype(np.float32),
        "fy": np.tile(np.random.uniform(0.05, 0.95, T), (P, 1)).astype(np.float32),
        "c00": striped(np.random.permutation(T)),
        "c01": striped(np.random.permutation(T)),
        "c10": striped(np.random.permutation(T)),
        "c11": striped(np.random.permutation(T)),
    }


def reference(x_words, x_scales, w1, fx, fy, c00, c01, c10, c11):
    xq = unpack_weight(x_words, x_scales)
    y = mxq(f64(w1), 0, "e4m3").T @ xq
    top = y[:, unstriped(c00)] + (y[:, unstriped(c01)] - y[:, unstriped(c00)]) * f64(fx)[:1]
    low = y[:, unstriped(c10)] + (y[:, unstriped(c11)] - y[:, unstriped(c10)]) * f64(fx)[:1]
    return top + (low - top) * f64(fy)[:1]

@@ -1,0 +1,178 @@
+from contextlib import ExitStack
+
+import concourse.mybir as mybir
+from concourse.masks import make_identity
+
+K, T, M = 512, 1024, 128
+FLOPS = 2 * K * T * M
+BYTES = K * T + (K // 32) * T + 4 * K * M + 2 * 4 * T + 4 * 2 * 128 * (T // 16) + 4 * M * T
+
+F32 = mybir.dt.float32
+BF16 = mybir.dt.bfloat16
+I32 = mybir.dt.int32
+U32 = mybir.dt.uint32
+U16 = mybir.dt.uint16
+U8 = mybir.dt.uint8
+FP8X4 = mybir.dt.float8_e4m3fn_x4
+COPY = mybir.ActivationFunctionType.Copy
+MULT = mybir.AluOpType.mult
+ADD = mybir.AluOpType.add
+
+P = 128
+BANK = 512
+BLOCKS = T // P
+MM_WIDTHS = (256, 256, 256, 128, 128)
+CHUNKS = (2, 2, 2, 1)
+
+
+def tile_picked_wbilin_none_l_kernel(tc, x_words, x_scales, w1, fx, fy, c00, c01, c10, c11, out):
+    nc = tc.nc
+    with ExitStack() as ctx:
+        keep = ctx.enter_context(tc.tile_pool(name="keep", bufs=1))
+        psum = ctx.enter_context(tc.psum_pool(name="psum", bufs=1))
+
+        def bank(i):
+            return psum.tile([P, BANK], F32, name="bank%d" % i, tag="bank%d" % i)
+
+        x_plane = keep.tile([P, T], U8, name="x_plane", align_bytes=64)
+        nc.gpsimd.memset(x_plane[:].bitcast(U32), 0)
+        w_raw = keep.tile([P, 4, M], F32, name="w_raw")
+        nc.sync.dma_start(out=w_raw[:], in_=w1.rearrange("(p j) m -> p j m", j=4))
+
+        x_flat = x_words[0].rearrange("p n t -> p (n t)").bitcast(I32)
+        x_codes = [keep.tile([P, BANK], U32, name="x_codes%d" % h, align_bytes=64) for h in range(2)]
+        nc.sync.dma_start(out=x_codes[0][:].bitcast(I32), in_=x_flat[:, 0:BANK])
+        for q in range(4):
+            nc.sync.dma_start(
+                out=x_plane[32 * q : 32 * q + 4, :].bitcast(I32),
+                in_=x_scales[0, 4 * q : 4 * q + 4, :].bitcast(I32),
+            )
+        nc.sync.dma_start(out=x_codes[1][:].bitcast(I32), in_=x_flat[:, BANK:T])
+
+        fx_rows = keep.tile([P, T], F32, name="fx_rows")
+        nc.sync.dma_start(out=fx_rows[:], in_=fx)
+
+        lists = {}
+        for name, src in (("c01", c01), ("c00", c00), ("c11", c11), ("c10", c10)):
+            lists[name] = keep.tile([P, T // 16], U16, name=name)
+            nc.sync.dma_start(lists[name][:], src)
+
+        ident = keep.tile([P, P], F32, name="ident")
+        make_identity(nc, ident[:])
+        fy_pieces = keep.tile([P, P], F32, name="fy_pieces")
+        nc.scalar.activation(fy_pieces[:], ident[:], COPY, scale=0.0)
+        nc.scalar.dma_start(out=fy_pieces[0:BLOCKS, :], in_=fy[0, :].rearrange("(b v) -> b v", v=P))
+
+        w_grouped = keep.tile([P, M, 4], BF16, name="w_grouped", align_bytes=64)
+        nc.vector.tensor_copy(
+            out=w_grouped[:].rearrange("p (c i) j -> p c j i", i=4),
+            in_=w_raw[:].rearrange("p j (c i) -> p c j i", i=4),
+        )
+        w_codes = keep.tile([P, M], U32, name="w_codes", align_bytes=64)
+        w_plane = keep.tile([P, M], U8, name="w_plane", align_bytes=64)
+        nc.vector.quantize_mx(
+            out=w_codes[:].bitcast(FP8X4), scales=w_plane[:], in_=w_grouped[:].rearrange("p m j -> p (m j)")
+        )
+
+        y = keep.tile([P, T], F32, name="y")
+        first = 0
+        for i, width in enumerate(MM_WIDTHS):
+            cols = slice(first, first + width)
+            codes = x_codes[first // BANK][:, first % BANK : first % BANK + width]
+            first = first + width
+            acc = bank(i)
+            nc.tensor.matmul_mx(
+                out=acc[:, 0:width],
+                lhsT=w_codes[:].bitcast(FP8X4),
+                lhsT_scale=w_plane[:],
+                rhs=codes.bitcast(FP8X4),
+                rhs_scale=x_plane[:, cols],
+                start=True,
+                stop=True,
+            )
+            if i % 2 == 0:
+                nc.scalar.copy(y[:, cols], acc[:, 0:width])
+            else:
+                nc.vector.tensor_copy(y[:, cols], acc[:, 0:width])
+
+        gx_rows = keep.tile([P, T], F32, name="gx_rows")
+
+        def gather(name, cols, weight, tag):
+            picked = keep.tile([P, cols.stop - cols.start], F32, name="%s_%s" % (name, tag))
+            offsets = lists[name][:, cols.start // 16 : cols.stop // 16]
+            nc.vector.tensor_tensor(picked[:], y[:].indirect(offsets), weight, MULT)
+            return picked
+
+        def add_transposed(dst, first, second):
+            nc.tensor.matmul(dst, first, ident[:], start=True, stop=False, is_transpose=True)
+            nc.tensor.matmul(dst, second, ident[:], start=False, stop=True, is_transpose=True)
+
+        def last_weights():
+            cols = slice(T - P, T)
+            b = BLOCKS - 1
+            nc.scalar.activation(gx_rows[:, cols], fx_rows[:, cols], COPY, scale=-1.0, bias=1.0)
+            turned = bank(6)
+            nc.tensor.transpose(turned[:, 0:P], fx_rows[:, cols], ident[:])
+            nc.tensor.transpose(turned[:, P : 2 * P], gx_rows[:, cols], ident[:])
+            w_t = keep.tile([P, 4, P], F32, name="w_t")
+            for n, (half, col) in enumerate(((0, gy_col), (1, gy_col), (0, fy_col), (1, fy_col))):
+                nc.scalar.activation(w_t[:, n, :], turned[:, half * P : (half + 1) * P], COPY, scale=col[:, b : b + 1])
+            back = bank(7)
+            for n in range(4):
+                nc.tensor.transpose(back[:, n * P : (n + 1) * P], w_t[:, n, :], ident[:])
+            w_last = keep.tile([P, 4 * P], F32, name="w_last")
+            nc.scalar.copy(w_last[:], back[:])
+            return w_last
+
+        start = 0
+        for c, nb in enumerate(CHUNKS):
+            cols = slice(start * P, (start + nb) * P)
+            nc.scalar.activation(gx_rows[:, cols], fx_rows[:, cols], COPY, scale=-1.0, bias=1.0)
+            start = start + nb
+
+        fy_t = bank(6)
+        nc.tensor.transpose(fy_t[:, 0:P], fy_pieces[:], ident[:])
+        fy_col = keep.tile([P, BLOCKS], F32, name="fy_col")
+        gy_col = keep.tile([P, BLOCKS], F32, name="gy_col")
+        nc.scalar.activation(gy_col[:], fy_t[:, 0:BLOCKS], COPY, scale=-1.0, bias=1.0)
+        nc.scalar.copy(fy_col[:], fy_t[:, 0:BLOCKS])
+
+        start = 0
+        for c, nb in enumerate(CHUNKS):
+            cols = slice(start * P, (start + nb) * P)
+            scaled = []
+            for h, (right, left, col) in enumerate((("c01", "c00", gy_col), ("c11", "c10", fy_col))):
+                g_right = gather(right, cols, fx_rows[:, cols], c)
+                g_left = gather(left, cols, gx_rows[:, cols], c)
+                turned = bank(3 * (c % 2) + h)
+                half = keep.tile([P, nb * P], F32, name="half_%d_%d" % (c, h))
+                for b in range(nb):
+                    blk = slice(b * P, (b + 1) * P)
+                    add_transposed(turned[:, blk], g_right[:, blk], g_left[:, blk])
+                for b in range(nb):
+                    blk = slice(b * P, (b + 1) * P)
+                    nc.scalar.activation(half[:, blk], turned[:, blk], COPY, scale=col[:, start + b : start + b + 1])
+                scaled.append(half)
+            back = bank(3 * (c % 2) + 2)
+            for b in range(nb):
+                blk = slice(b * P, (b + 1) * P)
+                add_transposed(back[:, blk], scaled[0][:, blk], scaled[1][:, blk])
+            result = keep.tile([P, nb * P], F32, name="result_%d" % c)
+            nc.scalar.copy(result[:], back[:, 0 : nb * P])
+            nc.sync.dma_start(out=out[:, cols], in_=result[:])
+            if c == 0:
+                w_last = last_weights()
+            start = start + nb
+
+        cols = slice(T - P, T)
+        g01 = gather("c01", cols, w_last[:, 0:P], "last")
+        g00 = gather("c00", cols, w_last[:, P : 2 * P], "last")
+        g11 = gather("c11", cols, w_last[:, 2 * P : 3 * P], "last")
+        top = keep.tile([P, P], F32, name="top_last")
+        nc.vector.tensor_tensor(top[:], g01[:], g00[:], ADD)
+        g10 = gather("c10", cols, w_last[:, 3 * P : 4 * P], "last")
+        three = keep.tile([P, P], F32, name="three_last")
+        nc.vector.tensor_tensor(three[:], top[:], g11[:], ADD)
+        result = keep.tile([P, P], F32, name="result_last")
+        nc.vector.tensor_tensor(result[:], three[:], g10[:], ADD)
+        nc.sync.dma_start(out=out[:, cols], in_=result[:])

@@ -22,7 +22,10 @@ P = 128
 BANK = 512
 BLOCKS = T // P
 MM_WIDTHS = (256, 256, 256, 128, 128)
-CHUNKS = (2, 2, 2, 1)
+
+
+def block_cols(first, count):
+    return slice(first * P, (first + count) * P)
 
 
 def tile_picked_wbilin_none_l_kernel(tc, x_words, x_scales, w1, fx, fy, c00, c01, c10, c11, out):
@@ -38,7 +41,6 @@ def tile_picked_wbilin_none_l_kernel(tc, x_words, x_scales, w1, fx, fy, c00, c01
         nc.gpsimd.memset(x_plane[:].bitcast(U32), 0)
         w_raw = keep.tile([P, 4, M], F32, name="w_raw")
         nc.sync.dma_start(out=w_raw[:], in_=w1.rearrange("(p j) m -> p j m", j=4))
-
         x_flat = x_words[0].rearrange("p n t -> p (n t)").bitcast(I32)
         x_codes = [keep.tile([P, BANK], U32, name="x_codes%d" % h, align_bytes=64) for h in range(2)]
         nc.sync.dma_start(out=x_codes[0][:].bitcast(I32), in_=x_flat[:, 0:BANK])
@@ -48,10 +50,11 @@ def tile_picked_wbilin_none_l_kernel(tc, x_words, x_scales, w1, fx, fy, c00, c01
                 in_=x_scales[0, 4 * q : 4 * q + 4, :].bitcast(I32),
             )
         nc.sync.dma_start(out=x_codes[1][:].bitcast(I32), in_=x_flat[:, BANK:T])
-
         fx_rows = keep.tile([P, T], F32, name="fx_rows")
         nc.sync.dma_start(out=fx_rows[:], in_=fx)
-
+        fy_pieces = keep.tile([P, P], F32, name="fy_pieces")
+        nc.vector.memset(fy_pieces[:], 0.0)
+        nc.sync.dma_start(out=fy_pieces[0:BLOCKS, :], in_=fy[0, :].rearrange("(b v) -> b v", v=P))
         lists = {}
         for name, src in (("c01", c01), ("c00", c00), ("c11", c11), ("c10", c10)):
             lists[name] = keep.tile([P, T // 16], U16, name=name)
@@ -59,9 +62,6 @@ def tile_picked_wbilin_none_l_kernel(tc, x_words, x_scales, w1, fx, fy, c00, c01
 
         ident = keep.tile([P, P], F32, name="ident")
         make_identity(nc, ident[:])
-        fy_pieces = keep.tile([P, P], F32, name="fy_pieces")
-        nc.scalar.activation(fy_pieces[:], ident[:], COPY, scale=0.0)
-        nc.scalar.dma_start(out=fy_pieces[0:BLOCKS, :], in_=fy[0, :].rearrange("(b v) -> b v", v=P))
 
         w_grouped = keep.tile([P, M, 4], BF16, name="w_grouped", align_bytes=64)
         nc.vector.tensor_copy(
@@ -78,14 +78,12 @@ def tile_picked_wbilin_none_l_kernel(tc, x_words, x_scales, w1, fx, fy, c00, c01
         first = 0
         for i, width in enumerate(MM_WIDTHS):
             cols = slice(first, first + width)
-            codes = x_codes[first // BANK][:, first % BANK : first % BANK + width]
-            first = first + width
             acc = bank(i)
             nc.tensor.matmul_mx(
                 out=acc[:, 0:width],
                 lhsT=w_codes[:].bitcast(FP8X4),
                 lhsT_scale=w_plane[:],
-                rhs=codes.bitcast(FP8X4),
+                rhs=x_codes[first // BANK][:, first % BANK : first % BANK + width].bitcast(FP8X4),
                 rhs_scale=x_plane[:, cols],
                 start=True,
                 stop=True,
@@ -94,85 +92,91 @@ def tile_picked_wbilin_none_l_kernel(tc, x_words, x_scales, w1, fx, fy, c00, c01
                 nc.scalar.copy(y[:, cols], acc[:, 0:width])
             else:
                 nc.vector.tensor_copy(y[:, cols], acc[:, 0:width])
+            first = first + width
 
         gx_rows = keep.tile([P, T], F32, name="gx_rows")
+        nc.vector.tensor_scalar(gx_rows[:, 0:BANK], fx_rows[:, 0:BANK], -1.0, 1.0, MULT, ADD)
+        nc.scalar.activation(gx_rows[:, BANK:T], fx_rows[:, BANK:T], COPY, scale=-1.0, bias=1.0)
 
-        def gather(name, cols, weight, tag):
-            picked = keep.tile([P, cols.stop - cols.start], F32, name="%s_%s" % (name, tag))
-            offsets = lists[name][:, cols.start // 16 : cols.stop // 16]
-            nc.vector.tensor_tensor(picked[:], y[:].indirect(offsets), weight, MULT)
-            return picked
-
-        def add_transposed(dst, first, second):
-            nc.tensor.matmul(dst, first, ident[:], start=True, stop=False, is_transpose=True)
-            nc.tensor.matmul(dst, second, ident[:], start=False, stop=True, is_transpose=True)
-
-        def last_weights():
-            cols = slice(T - P, T)
-            b = BLOCKS - 1
-            nc.scalar.activation(gx_rows[:, cols], fx_rows[:, cols], COPY, scale=-1.0, bias=1.0)
-            turned = bank(6)
-            nc.tensor.transpose(turned[:, 0:P], fx_rows[:, cols], ident[:])
-            nc.tensor.transpose(turned[:, P : 2 * P], gx_rows[:, cols], ident[:])
-            w_t = keep.tile([P, 4, P], F32, name="w_t")
-            for n, (half, col) in enumerate(((0, gy_col), (1, gy_col), (0, fy_col), (1, fy_col))):
-                nc.scalar.activation(w_t[:, n, :], turned[:, half * P : (half + 1) * P], COPY, scale=col[:, b : b + 1])
-            back = bank(7)
-            for n in range(4):
-                nc.tensor.transpose(back[:, n * P : (n + 1) * P], w_t[:, n, :], ident[:])
-            w_last = keep.tile([P, 4 * P], F32, name="w_last")
-            nc.scalar.copy(w_last[:], back[:])
-            return w_last
-
-        start = 0
-        for c, nb in enumerate(CHUNKS):
-            cols = slice(start * P, (start + nb) * P)
-            nc.scalar.activation(gx_rows[:, cols], fx_rows[:, cols], COPY, scale=-1.0, bias=1.0)
-            start = start + nb
-
-        fy_t = bank(6)
+        fy_t = bank(4)
         nc.tensor.transpose(fy_t[:, 0:P], fy_pieces[:], ident[:])
         fy_col = keep.tile([P, BLOCKS], F32, name="fy_col")
         gy_col = keep.tile([P, BLOCKS], F32, name="gy_col")
         nc.scalar.activation(gy_col[:], fy_t[:, 0:BLOCKS], COPY, scale=-1.0, bias=1.0)
         nc.scalar.copy(fy_col[:], fy_t[:, 0:BLOCKS])
 
-        start = 0
-        for c, nb in enumerate(CHUNKS):
-            cols = slice(start * P, (start + nb) * P)
-            scaled = []
-            for h, (right, left, col) in enumerate((("c01", "c00", gy_col), ("c11", "c10", fy_col))):
-                g_right = gather(right, cols, fx_rows[:, cols], c)
-                g_left = gather(left, cols, gx_rows[:, cols], c)
-                turned = bank(3 * (c % 2) + h)
-                half = keep.tile([P, nb * P], F32, name="half_%d_%d" % (c, h))
-                for b in range(nb):
-                    blk = slice(b * P, (b + 1) * P)
-                    add_transposed(turned[:, blk], g_right[:, blk], g_left[:, blk])
-                for b in range(nb):
-                    blk = slice(b * P, (b + 1) * P)
-                    nc.scalar.activation(half[:, blk], turned[:, blk], COPY, scale=col[:, start + b : start + b + 1])
-                scaled.append(half)
-            back = bank(3 * (c % 2) + 2)
-            for b in range(nb):
-                blk = slice(b * P, (b + 1) * P)
-                add_transposed(back[:, blk], scaled[0][:, blk], scaled[1][:, blk])
-            result = keep.tile([P, nb * P], F32, name="result_%d" % c)
-            nc.scalar.copy(result[:], back[:, 0 : nb * P])
-            nc.sync.dma_start(out=out[:, cols], in_=result[:])
-            if c == 0:
-                w_last = last_weights()
-            start = start + nb
+        def gather(picked, name, cols, weight):
+            offsets = lists[name][:, cols.start // 16 : cols.stop // 16]
+            nc.vector.tensor_tensor(picked, y[:].indirect(offsets), weight, MULT)
 
-        cols = slice(T - P, T)
-        g01 = gather("c01", cols, w_last[:, 0:P], "last")
-        g00 = gather("c00", cols, w_last[:, P : 2 * P], "last")
-        g11 = gather("c11", cols, w_last[:, 2 * P : 3 * P], "last")
-        top = keep.tile([P, P], F32, name="top_last")
-        nc.vector.tensor_tensor(top[:], g01[:], g00[:], ADD)
-        g10 = gather("c10", cols, w_last[:, 3 * P : 4 * P], "last")
-        three = keep.tile([P, P], F32, name="three_last")
-        nc.vector.tensor_tensor(three[:], top[:], g11[:], ADD)
-        result = keep.tile([P, P], F32, name="result_last")
-        nc.vector.tensor_tensor(result[:], three[:], g10[:], ADD)
+        def add_transposed(dst, terms):
+            for n, term in enumerate(terms):
+                nc.tensor.matmul(dst, term, ident[:], start=n == 0, stop=n == len(terms) - 1, is_transpose=True)
+
+        def turned_half(right, left, col, first, groups, g_right, g_left):
+            count = sum(size for size, i in groups)
+            cols = block_cols(first, count)
+            gather(g_right, right, cols, fx_rows[:, cols])
+            gather(g_left, left, cols, gx_rows[:, cols])
+            half = keep.tile([P, count * P], F32, name="half_%s_%d" % (right, first))
+            done = 0
+            for size, i in groups:
+                turned = bank(i)
+                for b in range(size):
+                    blk = block_cols(done + b, 1)
+                    add_transposed(turned[:, block_cols(b, 1)], (g_right[:, blk], g_left[:, blk]))
+                for b in range(size):
+                    at = first + done + b
+                    nc.scalar.activation(half[:, block_cols(done + b, 1)], turned[:, block_cols(b, 1)], COPY, scale=col[:, at : at + 1])
+                done = done + size
+            return [half[:, block_cols(b, 1)] for b in range(count)]
+
+        def finish(first, tops, lows, back):
+            count = len(lows)
+            for b in range(count):
+                add_transposed(back[:, block_cols(b, 1)], (tops[b], lows[b]))
+            result = keep.tile([P, count * P], F32, name="result_%d" % first)
+            nc.scalar.copy(result[:], back[:, 0 : count * P])
+            nc.sync.dma_start(out=out[:, block_cols(first, count)], in_=result[:])
+
+        turned = bank(3)
+        for b in range(2):
+            nc.tensor.transpose(turned[:, block_cols(2 * b, 1)], fx_rows[:, block_cols(b, 1)], ident[:])
+            nc.tensor.transpose(turned[:, block_cols(2 * b + 1, 1)], gx_rows[:, block_cols(b, 1)], ident[:])
+        w_t = keep.tile([P, BANK], F32, name="w_t")
+        for b in range(2):
+            nc.scalar.activation(w_t[:, block_cols(2 * b, 2)], turned[:, block_cols(2 * b, 2)], COPY, scale=fy_col[:, b : b + 1])
+        back = bank(7)
+        for side in range(2):
+            for b in range(2):
+                nc.tensor.transpose(back[:, block_cols(2 * side + b, 1)], w_t[:, block_cols(2 * b + side, 1)], ident[:])
+        w_low = keep.tile([P, BANK], F32, name="w_low")
+        nc.scalar.copy(w_low[:], back[:])
+
+        top_right = keep.tile([P, 4 * P], F32, name="top_right")
+        top_left = keep.tile([P, 4 * P], F32, name="top_left")
+        low_right = keep.tile([P, 2 * P], F32, name="low_right")
+        low_left = keep.tile([P, 2 * P], F32, name="low_left")
+        tops03 = turned_half("c01", "c00", gy_col, 0, ((2, 0), (2, 1)), top_right[:], top_left[:])
+        top_part = bank(5)
+        for b in range(2):
+            nc.tensor.transpose(top_part[:, block_cols(b, 1)], tops03[b], ident[:])
+        lows23 = turned_half("c11", "c10", fy_col, 2, ((1, 2), (1, 3)), low_right[:], low_left[:])
+        finish(2, tops03[2:4], lows23, bank(4))
+        tops47 = turned_half("c01", "c00", gy_col, 4, ((1, 2), (1, 3), (2, 4)), top_right[:], top_left[:])
+        lows45 = turned_half("c11", "c10", fy_col, 4, ((1, 2), (1, 3)), low_right[:], low_left[:])
+        lows6 = turned_half("c11", "c10", fy_col, 6, ((1, 4),), tops03[2], lows23[0])
+        lows7 = turned_half("c11", "c10", fy_col, 7, ((1, 2),), tops03[3], lows23[1])
+        finish(4, tops47[0:2], lows45, bank(0))
+        finish(6, tops47[2:4], lows6 + lows7, bank(1))
+
+        cols = block_cols(0, 2)
+        g11 = top_right[:, block_cols(2, 2)]
+        g10 = top_left[:, block_cols(2, 2)]
+        gather(g11, "c11", cols, w_low[:, block_cols(0, 2)])
+        gather(g10, "c10", cols, w_low[:, block_cols(2, 2)])
+        three = keep.tile([P, 2 * P], F32, name="three")
+        nc.vector.tensor_tensor(three[:], g11, top_part[:, 0 : 2 * P], ADD)
+        result = keep.tile([P, 2 * P], F32, name="result_0")
+        nc.vector.tensor_tensor(result[:], three[:], g10, ADD)
         nc.sync.dma_start(out=out[:, cols], in_=result[:])

from contextlib import ExitStack

import concourse.mybir as mybir
from concourse.masks import make_identity

K, T, M = 512, 1024, 128
FLOPS = 2 * K * T * M
BYTES = K * T + (K // 32) * T + 4 * K * M + 2 * 4 * T + 4 * 2 * 128 * (T // 16) + 4 * M * T

F32 = mybir.dt.float32
BF16 = mybir.dt.bfloat16
I32 = mybir.dt.int32
U32 = mybir.dt.uint32
U16 = mybir.dt.uint16
U8 = mybir.dt.uint8
FP8X4 = mybir.dt.float8_e4m3fn_x4
COPY = mybir.ActivationFunctionType.Copy
MULT = mybir.AluOpType.mult
ADD = mybir.AluOpType.add

P = 128
BANK = 512
BLOCKS = T // P
MM_WIDTHS = (256, 256, 256, 128, 128)


def block_cols(first, count):
    return slice(first * P, (first + count) * P)


def tile_picked_wbilin_none_l_kernel(tc, x_words, x_scales, w1, fx, fy, c00, c01, c10, c11, out):
    nc = tc.nc
    with ExitStack() as ctx:
        keep = ctx.enter_context(tc.tile_pool(name="keep", bufs=1))
        psum = ctx.enter_context(tc.psum_pool(name="psum", bufs=1))

        def bank(i):
            return psum.tile([P, BANK], F32, name="bank%d" % i, tag="bank%d" % i)

        x_plane = keep.tile([P, T], U8, name="x_plane", align_bytes=64)
        nc.gpsimd.memset(x_plane[:].bitcast(U32), 0)
        w_raw = keep.tile([P, 4, M], F32, name="w_raw")
        nc.sync.dma_start(out=w_raw[:], in_=w1.rearrange("(p j) m -> p j m", j=4))
        x_flat = x_words[0].rearrange("p n t -> p (n t)").bitcast(I32)
        x_codes = [keep.tile([P, BANK], U32, name="x_codes%d" % h, align_bytes=64) for h in range(2)]
        nc.sync.dma_start(out=x_codes[0][:].bitcast(I32), in_=x_flat[:, 0:BANK])
        for q in range(4):
            nc.sync.dma_start(
                out=x_plane[32 * q : 32 * q + 4, :].bitcast(I32),
                in_=x_scales[0, 4 * q : 4 * q + 4, :].bitcast(I32),
            )
        nc.sync.dma_start(out=x_codes[1][:].bitcast(I32), in_=x_flat[:, BANK:T])
        fx_rows = keep.tile([P, T], F32, name="fx_rows")
        nc.sync.dma_start(out=fx_rows[:], in_=fx)
        fy_pieces = keep.tile([P, P], F32, name="fy_pieces")
        nc.vector.memset(fy_pieces[:], 0.0)
        nc.sync.dma_start(out=fy_pieces[0:BLOCKS, :], in_=fy[0, :].rearrange("(b v) -> b v", v=P))
        lists = {}
        for name, src in (("c01", c01), ("c00", c00), ("c11", c11), ("c10", c10)):
            lists[name] = keep.tile([P, T // 16], U16, name=name)
            nc.sync.dma_start(lists[name][:], src)

        ident = keep.tile([P, P], F32, name="ident")
        make_identity(nc, ident[:])

        w_grouped = keep.tile([P, M, 4], BF16, name="w_grouped", align_bytes=64)
        nc.vector.tensor_copy(
            out=w_grouped[:].rearrange("p (c i) j -> p c j i", i=4),
            in_=w_raw[:].rearrange("p j (c i) -> p c j i", i=4),
        )
        w_codes = keep.tile([P, M], U32, name="w_codes", align_bytes=64)
        w_plane = keep.tile([P, M], U8, name="w_plane", align_bytes=64)
        nc.vector.quantize_mx(
            out=w_codes[:].bitcast(FP8X4), scales=w_plane[:], in_=w_grouped[:].rearrange("p m j -> p (m j)")
        )

        y = keep.tile([P, T], F32, name="y")
        first = 0
        for i, width in enumerate(MM_WIDTHS):
            cols = slice(first, first + width)
            acc = bank(i)
            nc.tensor.matmul_mx(
                out=acc[:, 0:width],
                lhsT=w_codes[:].bitcast(FP8X4),
                lhsT_scale=w_plane[:],
                rhs=x_codes[first // BANK][:, first % BANK : first % BANK + width].bitcast(FP8X4),
                rhs_scale=x_plane[:, cols],
                start=True,
                stop=True,
            )
            if i % 2 == 0:
                nc.scalar.copy(y[:, cols], acc[:, 0:width])
            else:
                nc.vector.tensor_copy(y[:, cols], acc[:, 0:width])
            first = first + width

        gx_rows = keep.tile([P, T], F32, name="gx_rows")
        nc.vector.tensor_scalar(gx_rows[:, 0:BANK], fx_rows[:, 0:BANK], -1.0, 1.0, MULT, ADD)
        nc.scalar.activation(gx_rows[:, BANK:T], fx_rows[:, BANK:T], COPY, scale=-1.0, bias=1.0)

        fy_t = bank(4)
        nc.tensor.transpose(fy_t[:, 0:P], fy_pieces[:], ident[:])
        fy_col = keep.tile([P, BLOCKS], F32, name="fy_col")
        gy_col = keep.tile([P, BLOCKS], F32, name="gy_col")
        nc.scalar.activation(gy_col[:], fy_t[:, 0:BLOCKS], COPY, scale=-1.0, bias=1.0)
        nc.scalar.copy(fy_col[:], fy_t[:, 0:BLOCKS])

        def gather(picked, name, cols, weight):
            offsets = lists[name][:, cols.start // 16 : cols.stop // 16]
            nc.vector.tensor_tensor(picked, y[:].indirect(offsets), weight, MULT)

        def add_transposed(dst, terms):
            for n, term in enumerate(terms):
                nc.tensor.matmul(dst, term, ident[:], start=n == 0, stop=n == len(terms) - 1, is_transpose=True)

        def turned_half(right, left, col, first, groups, g_right, g_left):
            count = sum(size for size, i in groups)
            cols = block_cols(first, count)
            gather(g_right, right, cols, fx_rows[:, cols])
            gather(g_left, left, cols, gx_rows[:, cols])
            half = keep.tile([P, count * P], F32, name="half_%s_%d" % (right, first))
            done = 0
            for size, i in groups:
                turned = bank(i)
                for b in range(size):
                    blk = block_cols(done + b, 1)
                    add_transposed(turned[:, block_cols(b, 1)], (g_right[:, blk], g_left[:, blk]))
                for b in range(size):
                    at = first + done + b
                    nc.scalar.activation(half[:, block_cols(done + b, 1)], turned[:, block_cols(b, 1)], COPY, scale=col[:, at : at + 1])
                done = done + size
            return [half[:, block_cols(b, 1)] for b in range(count)]

        def finish(first, tops, lows, back):
            count = len(lows)
            for b in range(count):
                add_transposed(back[:, block_cols(b, 1)], (tops[b], lows[b]))
            result = keep.tile([P, count * P], F32, name="result_%d" % first)
            nc.scalar.copy(result[:], back[:, 0 : count * P])
            nc.sync.dma_start(out=out[:, block_cols(first, count)], in_=result[:])

        turned = bank(3)
        for b in range(2):
            nc.tensor.transpose(turned[:, block_cols(2 * b, 1)], fx_rows[:, block_cols(b, 1)], ident[:])
            nc.tensor.transpose(turned[:, block_cols(2 * b + 1, 1)], gx_rows[:, block_cols(b, 1)], ident[:])
        w_t = keep.tile([P, BANK], F32, name="w_t")
        for b in range(2):
            nc.scalar.activation(w_t[:, block_cols(2 * b, 2)], turned[:, block_cols(2 * b, 2)], COPY, scale=fy_col[:, b : b + 1])
        back = bank(7)
        for side in range(2):
            for b in range(2):
                nc.tensor.transpose(back[:, block_cols(2 * side + b, 1)], w_t[:, block_cols(2 * b + side, 1)], ident[:])
        w_low = keep.tile([P, BANK], F32, name="w_low")
        nc.scalar.copy(w_low[:], back[:])

        top_right = keep.tile([P, 4 * P], F32, name="top_right")
        top_left = keep.tile([P, 4 * P], F32, name="top_left")
        low_right = keep.tile([P, 2 * P], F32, name="low_right")
        low_left = keep.tile([P, 2 * P], F32, name="low_left")
        tops03 = turned_half("c01", "c00", gy_col, 0, ((2, 0), (2, 1)), top_right[:], top_left[:])
        top_part = bank(5)
        for b in range(2):
            nc.tensor.transpose(top_part[:, block_cols(b, 1)], tops03[b], ident[:])
        lows23 = turned_half("c11", "c10", fy_col, 2, ((1, 2), (1, 3)), low_right[:], low_left[:])
        finish(2, tops03[2:4], lows23, bank(4))
        tops47 = turned_half("c01", "c00", gy_col, 4, ((1, 2), (1, 3), (2, 4)), top_right[:], top_left[:])
        lows45 = turned_half("c11", "c10", fy_col, 4, ((1, 2), (1, 3)), low_right[:], low_left[:])
        lows6 = turned_half("c11", "c10", fy_col, 6, ((1, 4),), tops03[2], lows23[0])
        lows7 = turned_half("c11", "c10", fy_col, 7, ((1, 2),), tops03[3], lows23[1])
        finish(4, tops47[0:2], lows45, bank(0))
        finish(6, tops47[2:4], lows6 + lows7, bank(1))

        cols = block_cols(0, 2)
        g11 = top_right[:, block_cols(2, 2)]
        g10 = top_left[:, block_cols(2, 2)]
        gather(g11, "c11", cols, w_low[:, block_cols(0, 2)])
        gather(g10, "c10", cols, w_low[:, block_cols(2, 2)])
        three = keep.tile([P, 2 * P], F32, name="three")
        nc.vector.tensor_tensor(three[:], g11, top_part[:, 0 : 2 * P], ADD)
        result = keep.tile([P, 2 * P], F32, name="result_0")
        nc.vector.tensor_tensor(result[:], three[:], g10, ADD)
        nc.sync.dma_start(out=out[:, cols], in_=result[:])
